import numpy as np
import ml_dtypes


def mxq(x, axis, fmt="e4m3"):
    dtype, down = {"e4m3": (ml_dtypes.float8_e4m3fn, 7), "e5m2": (ml_dtypes.float8_e5m2, 14)}[fmt]
    v = np.moveaxis(np.asarray(x, np.float32).astype(ml_dtypes.bfloat16).astype(np.float64), axis, -1)
    blocks = v.reshape(v.shape[:-1] + (-1, 32))
    amax = np.abs(blocks).max(-1, keepdims=True)
    byte = np.maximum(np.where(amax > 0, np.frexp(amax)[1] - 1 + 127, 0) - down, 1)
    scale = np.exp2(byte - 127.0)
    codes = (blocks / scale).astype(np.float32).astype(dtype).astype(np.float64)
    return np.moveaxis((codes * scale).reshape(v.shape), -1, axis)


WIDE = False


def mx_kscale(k):
    if not WIDE:
        return np.ones(k)
    levels = np.array([10, -10, 5, -5, 0])
    if k % 512:
        return np.exp2(np.random.permutation(np.resize(levels, k // 32))).repeat(32)
    a = np.empty((k // 512, 16))
    for p in range(k // 512):
        a[p, :8] = np.random.permutation(np.resize(levels, 8))
        for g in range(8):
            far = levels[np.abs(levels - a[p, g]) >= 10]
            a[p, g + 8] = far[np.random.randint(len(far))]
    return np.exp2(a.ravel()).repeat(32)


def f64(x):
    return np.asarray(x).astype(np.float64)


def striped(idx):
    return np.tile(np.asarray(idx).reshape(-1, 16).T, (8, 1)).astype(np.uint16)


def unstriped(offs):
    return offs[:16].T.reshape(-1).astype(np.int64)


E2M1 = np.array([0.0, 0.5, 1.0, 1.5, 2.0, 3.0, 4.0, 6.0, -0.0, -0.5, -1.0, -1.5, -2.0, -3.0, -4.0, -6.0])


def pack_weight(w, fmt):
    k, n = w.shape
    w = f64(np.asarray(w, np.float32).astype(ml_dtypes.bfloat16)).reshape(k // 32, 32, n)
    amax = np.abs(w).max(1)
    if fmt == "e4m3":
        byte = np.frexp(amax)[1] - 1 + 127 - 7
    else:
        mant, ex = np.frexp(amax / 6.0)
        byte = np.where(mant > 0.5, ex, ex - 1) + 127
    byte = np.clip(np.where(amax > 0, byte, 1), 1, 254)
    scaled = (w * np.exp2(127.0 - byte)[:, None, :]).reshape(k, n).astype(np.float32)
    by_word = np.ascontiguousarray(scaled.reshape(k // 512, 128, 4, n).transpose(0, 1, 3, 2))
    if fmt == "e4m3":
        words = by_word.astype(ml_dtypes.float8_e4m3fn).view(np.uint8)
    else:
        c = by_word.astype(ml_dtypes.float4_e2m1fn).view(np.uint8) & 0xF
        words = (c[..., 0::2] | (c[..., 1::2] << 4)).reshape(k // 512, 128, 2 * n)
    return np.ascontiguousarray(words), np.ascontiguousarray(byte.astype(np.uint8).reshape(k // 512, 16, n))


def unpack_weight(words, scales, fmt):
    g, _, n = scales.shape
    words = np.ascontiguousarray(words).reshape(g, 128, n, -1)
    if fmt == "e4m3":
        vals = words.view(ml_dtypes.float8_e4m3fn).astype(np.float64)
    else:
        nib = np.empty((g, 128, n, 4), np.uint8)
        nib[..., 0::2] = words & 0xF
        nib[..., 1::2] = words >> 4
        vals = E2M1[nib]
    vals = vals * np.repeat(np.exp2(scales.astype(np.float64) - 127.0), 8, axis=1)[..., None]
    return vals.transpose(0, 1, 3, 2).reshape(g * 512, n)


def silu(v):
    return v / (1.0 + np.exp(-v))


def bf(x):
    return np.asarray(x, np.float32).astype(ml_dtypes.bfloat16)


def planes(Y):
    r, m = Y.shape
    b = f64(bf(Y)).reshape(r // 32, 32, m)
    amax = np.abs(b).max(1)
    byte = np.clip(np.where(amax > 0, np.frexp(amax)[1] - 1 + 127 - 7, 1), 1, 254)
    codes = (b * np.exp2(127.0 - byte)[:, None, :]).reshape(r, m).astype(np.float32).astype(ml_dtypes.float8_e4m3fn).view(np.uint8)
    words = codes.reshape(r // 512, 128, 4, m).transpose(0, 1, 3, 2)
    return np.ascontiguousarray(words), np.ascontiguousarray(byte.astype(np.uint8).reshape(r // 512, 16, m))


B, N, T, D, NQ = 1, 512, 2048, 1024, 512
DV = 512


def sgn(shape):
    return np.random.uniform(0.5, 2.0, shape) * np.where(np.random.standard_normal(shape) < 0, -1.0, 1.0)


def setup_inputs():
    n = np.random.standard_normal
    idx = np.random.permutation(T)[:B * N]
    s = mx_kscale(D)[:, None]
    u = mx_kscale(N)
    ut = np.ones(T)
    ut[idx] = u
    kp = pack_weight(n((D, T)) / s, "e2m1")
    return {
        "qT": (n((B, D, NQ)) * s * (1.00 / np.sqrt(D))).astype(np.float32),
        "k_words": np.ascontiguousarray(kp[0].reshape(1, 2, 128, T, 2).transpose(0, 2, 3, 1, 4)).reshape(1, 128, T, 4),
        "k_scales": kp[1],
        "vT": (n((DV, T)) / ut).astype(np.float32),
        "ob": (0.5 * n((B, DV, 1))).astype(np.float32),
        "us": (sgn((B, N, 1)) * u[:, None]).astype(np.float32),
        "offs": striped(idx),
    }


def reference(qT, k_words, k_scales, vT, ob, us, offs):
    idx = unstriped(offs)
    pick = lambda x, which: x[:, which].reshape(x.shape[0], B, -1).transpose(1, 0, 2)
    k = unpack_weight(k_words.reshape(1, 128, T, 2, 2).transpose(0, 3, 1, 2, 4).reshape(2, 128, 2 * T), k_scales, "e2m1")
    kg = pick(k, idx)
    qq = mxq(f64(qT), 1, "e4m3")
    a = kg.transpose(0, 2, 1) @ qq
    y = silu(a) * f64(us)
    wq = mxq(y, 1, "e4m3")
    o = mxq(pick(f64(vT), idx).transpose(0, 2, 1), 1, "e4m3").transpose(0, 2, 1) @ wq
    r_ = o + f64(ob)
    Y = r_[0]
    words, scales = planes(Y)
    return Y, words, scales

@@ -1,0 +1,210 @@
+from contextlib import ExitStack
+
+import concourse.mybir as mybir
+from concourse.masks import make_identity
+
+F32 = mybir.dt.float32
+BF16 = mybir.dt.bfloat16
+I32 = mybir.dt.int32
+U32 = mybir.dt.uint32
+U16 = mybir.dt.uint16
+U8 = mybir.dt.uint8
+FP8X4 = mybir.dt.float8_e4m3fn_x4
+FP4X4 = mybir.dt.float4_e2m1fn_x4
+ACT = mybir.ActivationFunctionType
+ALU = mybir.AluOpType
+
+P = 128
+PACK = 4
+SLOTS, TOKENS, D, NQ, DV = 512, 2048, 1024, 512, 512
+PASSES = D // (P * PACK)
+CHUNK = 128
+CHUNKS = NQ // CHUNK
+HALF = NQ // 2
+
+FLOPS = 2 * SLOTS * NQ * (D + DV)
+
+
+def tile_attend_plo_mlpsilu_topk_kernel(tc, qT, k_words, k_scales, vT, ob, us, offs, out_0, out_1, out_2):
+    nc = tc.nc
+    with ExitStack() as ctx:
+        sb = ctx.enter_context(tc.tile_pool(name="sb", bufs=1))
+        reuse = ctx.enter_context(tc.tile_pool(name="reuse", bufs=1))
+        ps = ctx.enter_context(tc.psum_pool(name="ps", bufs=1))
+
+        def tile(shape, dtype, name, tag=None):
+            return sb.tile(shape, dtype, name=name, tag=tag or name, align_bytes=64)
+
+        def placed(shape, dtype, name, offset):
+            return reuse.tile(shape, dtype, name=name, align_bytes=64, offset=offset)
+
+        def weave(engine_copy, dst, src):
+            engine_copy(dst.rearrange("p (c i) t -> p c t i", i=4), src.rearrange("p t (c i) -> p c t i", i=4))
+
+        offsets = sb.tile([P, SLOTS // 16], U16, name="offsets")
+        nc.sync.dma_start(offsets[:], offs)
+        k_pool = tile([P, TOKENS], I32, "k_pool")
+        nc.sync.dma_start(k_pool[:], k_words[0].rearrange("p t b -> p (t b)").bitcast(I32))
+        ks_pool = tile([P, TOKENS], U8, "ks_pool")
+        nc.vector.memset(ks_pool[:].bitcast(I32), 0)
+        for j in range(4):
+            nc.sync.dma_start(ks_pool[j:P:16, :].bitcast(I32), k_scales[:, j:16:4, :].rearrange("o f t -> f o t").bitcast(I32))
+        q_raw = [tile([P, PACK, NQ], F32, f"q_raw{o}") for o in range(PASSES)]
+        q_rows = qT[0].rearrange("(o p j) w -> o p j w", o=PASSES, j=PACK)
+        for o in range(PASSES):
+            nc.sync.dma_start(q_raw[o][:], q_rows[o])
+        v_rows = vT.rearrange("(p u) t -> p u t", u=PACK)
+        v_pool = {}
+
+        def load_v(u, tag):
+            v_pool[u] = placed([P, TOKENS], F32, "v_pool2", 0) if u == 2 else tile([P, TOKENS], F32, f"v_pool{u}", tag)
+            nc.sync.dma_start(v_pool[u][:], v_rows[:, u, :])
+
+        load_v(0, None)
+        us_t = tile([P, PACK], F32, "us_t")
+        nc.sync.dma_start(us_t[:], us[0].rearrange("(p r) o -> p (r o)", r=PACK))
+        ob_t = tile([P, PACK], F32, "ob_t")
+        nc.sync.dma_start(ob_t[:], ob[0].rearrange("(p r) o -> p (r o)", r=PACK))
+        for u in range(1, PACK):
+            load_v(u, None)
+        ks_moved = tile([P, SLOTS], U8, "ks_moved")
+        nc.gpsimd.memset(ks_moved[:].bitcast(I32), 0)
+        ident = tile([P, P], F32, "ident")
+        make_identity(nc, ident[:])
+
+        k_got = tile([P, SLOTS], I32, "k_got")
+        nc.vector.tensor_copy(k_got[:].bitcast(U32), k_pool[:].bitcast(U32).indirect(offsets[:]))
+        ks_both = tile([P, SLOTS], U8, "ks_both")
+        nc.vector.tensor_copy(ks_both[:].rearrange("p (r s) -> p s r", r=PACK), ks_pool[:].indirect(offsets[:]))
+        nc.gpsimd.dma_start(ks_moved[0:100, :].bitcast(I32), ks_both[16:116, :].bitcast(I32))
+        ks_dealt = [ks_both, ks_moved]
+        k_dealt = []
+        k_halves = k_got[:].bitcast(U16).rearrange("p (a i r o) -> p o a r i", i=4, r=PACK, o=PASSES)
+
+        def split_k(o, tag):
+            k_dealt.append(tile([P, 2 * SLOTS], U8, f"k_dealt{o}", tag))
+            nc.vector.tensor_copy(k_dealt[o][:].bitcast(U16).rearrange("p (r a i) -> p a r i", r=PACK, i=4), k_halves[:, o])
+
+        split_k(0, "ks_pool")
+
+        q_codes, q_scales = {}, {}
+
+        def quantize_q(o, copies):
+            q_bf = [tile([P, HALF, PACK], BF16, f"q_bf{o}{h}") for h in range(2)]
+            for h in range(2):
+                weave(copies[h], q_bf[h][:], q_raw[o][:, :, HALF * h : HALF * (h + 1)])
+            for h in range(2):
+                q_codes[o, h] = tile([P, HALF], U32, f"q_codes{o}{h}")
+                q_scales[o, h] = tile([P, HALF], U8, f"q_scales{o}{h}")
+                nc.vector.quantize_mx(out=q_codes[o, h][:].bitcast(FP8X4), scales=q_scales[o, h][:],
+                                      in_=q_bf[h][:].rearrange("p n t -> p (n t)"))
+
+        quantize_q(0, [nc.vector.tensor_copy, nc.vector.tensor_copy])
+        split_k(1, "q_bf00")
+        quantize_q(1, [nc.vector.tensor_copy, nc.vector.tensor_copy])
+
+        a_banks = [ps.tile([P, PACK, CHUNK], F32, name=f"a_bank{c}", tag=f"bank{c}") for c in range(CHUNKS)]
+        for o in range(PASSES):
+            for c in range(CHUNKS):
+                h, cols = c // 2, slice(CHUNK * (c % 2), CHUNK * (c % 2 + 1))
+                for r in range(PACK):
+                    nc.tensor.matmul_mx(
+                        out=a_banks[c][:, r, :],
+                        lhsT=k_dealt[o][:, 2 * P * r : 2 * P * (r + 1)].bitcast(FP4X4),
+                        lhsT_scale=ks_dealt[o][:, P * r : P * (r + 1)],
+                        rhs=q_codes[o, h][:, cols].bitcast(FP8X4),
+                        rhs_scale=q_scales[o, h][:, cols],
+                        start=(o == 0 and r == 0),
+                        stop=(o == PASSES - 1 and r == PACK - 1),
+                    )
+
+        v_codes, v_scales = {}, {}
+
+        def gather_v(u, on_vector):
+            v_got = tile([P, SLOTS], BF16, f"v_got{u}")
+            if on_vector > 0:
+                nc.vector.tensor_copy(v_got[:, 0:on_vector], v_pool[u][:].indirect(offsets[:, 0 : on_vector // 16]))
+            if on_vector < SLOTS:
+                nc.scalar.activation(v_got[:, on_vector:SLOTS], v_pool[u][:].indirect(offsets[:, on_vector // 16 : SLOTS // 16]), ACT.Copy)
+            return v_got
+
+        def turn_v(u, v_got, v_bf):
+            words = v_got[:].bitcast(F32)
+            turned = ps.tile([P, 2, P], F32, name=f"turned{u}", tag=("bank0", "bank6", "bank7", "bank6")[u])
+            for h in range(2):
+                nc.tensor.transpose(turned[:, h, :], words[:, h : SLOTS // 2 : 2], ident[:])
+            nc.scalar.copy(v_bf.rearrange("p (m h) -> p m h", h=2), turned[:].rearrange("p h m -> p m h"))
+
+        def quantize_v(us_here, v_bf, tag=None):
+            codes = tile([P, P * len(us_here)], U32, f"v_codes{us_here[0]}", tag)
+            scales = tile([P, P * len(us_here)], U8, f"v_scales{us_here[0]}")
+            nc.vector.quantize_mx(out=codes[:].bitcast(FP8X4), scales=scales[:], in_=v_bf[:].bitcast(BF16))
+            for n, u in enumerate(us_here):
+                v_codes[u], v_scales[u] = codes[:, P * n : P * (n + 1)], scales[:, P * n : P * (n + 1)]
+
+        v_got0 = gather_v(0, SLOTS)
+
+        y_bf = tile([P, NQ * PACK], BF16, "y_bf", "v_pool0")
+        y_codes = tile([P, NQ], U32, "y_codes")
+        y_scales = tile([P, NQ], U8, "y_scales")
+        us_wide = us_t[:].unsqueeze(1).to_broadcast([P, CHUNK, PACK])
+        for c in range(CHUNKS):
+            act = tile([P, CHUNK, PACK], F32, f"act{c}")
+            nc.scalar.activation(act[:], a_banks[c][:].rearrange("p r n -> p n r"), ACT.Silu)
+            nc.vector.tensor_tensor(y_bf[:, PACK * CHUNK * c : PACK * CHUNK * (c + 1)].rearrange("p (n t) -> p n t", t=PACK), act[:], us_wide, ALU.mult)
+        v_got1 = gather_v(1, 0)
+        for h in range(2):
+            cols = slice(HALF * h, HALF * (h + 1))
+            nc.vector.quantize_mx(out=y_codes[:, cols].bitcast(FP8X4), scales=y_scales[:, cols],
+                                  in_=y_bf[:, PACK * cols.start : PACK * cols.stop])
+
+        res = placed([P, PACK * NQ], F32, "res", 2048)
+        res_rows = res[:].rearrange("p (u q) -> p u q", u=PACK)
+        out_rows = out_0.rearrange("(p u) q -> p u q", u=PACK)
+
+        def second(u, cols, tag, on_vector):
+            bank = ps.tile([P, cols.stop - cols.start], F32, name=f"o_bank{u}_{cols.start}", tag=tag)
+            nc.tensor.matmul_mx(out=bank[:], lhsT=v_codes[u].bitcast(FP8X4), lhsT_scale=v_scales[u],
+                                rhs=y_codes[:, cols].bitcast(FP8X4), rhs_scale=y_scales[:, cols], start=True, stop=True)
+            if on_vector:
+                nc.vector.tensor_scalar(res[:, NQ * u + cols.start : NQ * u + cols.stop], bank[:], ob_t[:, u : u + 1], None, ALU.add)
+            else:
+                nc.scalar.activation(res[:, NQ * u + cols.start : NQ * u + cols.stop], bank[:], ACT.Identity, bias=ob_t[:, u : u + 1])
+
+        def store(u):
+            nc.sync.dma_start(out_rows[:, u, :], res[:, u * NQ : (u + 1) * NQ])
+
+        whole = slice(0, NQ)
+        v_bf0 = tile([P, 2 * P], F32, "v_bf0")
+        turn_v(0, v_got0, v_bf0[:])
+        quantize_v([0], v_bf0)
+        v_got2 = gather_v(2, HALF)
+        second(0, whole, "bank4", True)
+        store(0)
+        v_bf12 = placed([P, 4 * P], F32, "v_bf12", 0)
+        turn_v(1, v_got1, v_bf12[:, 0 : 2 * P])
+        turn_v(2, v_got2, v_bf12[:, 2 * P : 4 * P])
+        v_got3 = gather_v(3, HALF)
+        quantize_v([1, 2], v_bf12, "v_pool3")
+        v_bf3 = tile([P, 2 * P], F32, "v_bf3")
+        turn_v(3, v_got3, v_bf3[:])
+        quantize_v([3], v_bf3)
+        second(1, whole, "bank5", False)
+        store(1)
+        second(2, whole, "bank1", True)
+        store(2)
+        second(3, slice(0, HALF), "bank2", False)
+        second(3, slice(HALF, NQ), "bank3", True)
+        store(3)
+
+        res_bf = tile([P, NQ, PACK], BF16, "res_bf")
+        o_codes = tile([P, NQ], I32, "o_codes")
+        o_scales = tile([P, NQ], U8, "o_scales")
+        weave(nc.vector.tensor_copy, res_bf[:, 0:HALF, :], res_rows[:, :, 0:HALF])
+        weave(nc.vector.tensor_copy, res_bf[:, HALF : HALF + CHUNK, :], res_rows[:, :, HALF : HALF + CHUNK])
+        weave(nc.scalar.copy, res_bf[:, HALF + CHUNK : NQ, :], res_rows[:, :, HALF + CHUNK : NQ])
+        nc.vector.quantize_mx(out=o_codes[:].bitcast(FP8X4), scales=o_scales[:], in_=res_bf[:].rearrange("p n t -> p (n t)"))
+        nc.sync.dma_start(out_1[0].rearrange("p q b -> p (q b)").bitcast(I32), o_codes[:])
+        for j in range(4):
+            engine = nc.scalar if j % 2 else nc.sync
+            engine.dma_start(out_2[0, j:16:4, :].bitcast(I32), o_scales[j:P:32, :].bitcast(I32))

@@ -49,7 +49,7 @@ def tile_attend_plo_mlpsilu_topk_kernel(tc, qT, k_words, k_scales, vT, ob, us, o
         nc.vector.memset(ks_pool[:].bitcast(I32), 0)
         for j in range(4):
             nc.sync.dma_start(ks_pool[j:P:16, :].bitcast(I32), k_scales[:, j:16:4, :].rearrange("o f t -> f o t").bitcast(I32))
-        q_raw = [tile([P, PACK, NQ], F32, f"q_raw{o}") for o in range(PASSES)]
+        q_raw = [placed([P, PACK, NQ], F32, "q_raw0", 0), tile([P, PACK, NQ], F32, "q_raw1")]
         q_rows = qT[0].rearrange("(o p j) w -> o p j w", o=PASSES, j=PACK)
         for o in range(PASSES):
             nc.sync.dma_start(q_raw[o][:], q_rows[o])
@@ -65,8 +65,6 @@ def tile_attend_plo_mlpsilu_topk_kernel(tc, qT, k_words, k_scales, vT, ob, us, o
         nc.sync.dma_start(us_t[:], us[0].rearrange("(p r) o -> p (r o)", r=PACK))
         ob_t = tile([P, PACK], F32, "ob_t")
         nc.sync.dma_start(ob_t[:], ob[0].rearrange("(p r) o -> p (r o)", r=PACK))
-        for u in range(1, PACK):
-            load_v(u, None)
         ks_moved = tile([P, SLOTS], U8, "ks_moved")
         nc.gpsimd.memset(ks_moved[:].bitcast(I32), 0)
         ident = tile([P, P], F32, "ident")
@@ -74,10 +72,13 @@ def tile_attend_plo_mlpsilu_topk_kernel(tc, qT, k_words, k_scales, vT, ob, us, o
 
         k_got = tile([P, SLOTS], I32, "k_got")
         nc.vector.tensor_copy(k_got[:].bitcast(U32), k_pool[:].bitcast(U32).indirect(offsets[:]))
+        ks_got = tile([P, SLOTS], U8, "ks_got")
+        nc.vector.tensor_copy(ks_got[:], ks_pool[:].indirect(offsets[:]))
         ks_both = tile([P, SLOTS], U8, "ks_both")
-        nc.vector.tensor_copy(ks_both[:].rearrange("p (r s) -> p s r", r=PACK), ks_pool[:].indirect(offsets[:]))
-        nc.gpsimd.dma_start(ks_moved[0:100, :].bitcast(I32), ks_both[16:116, :].bitcast(I32))
+        nc.vector.tensor_copy(ks_both[:].rearrange("p (r s) -> p r s", r=PACK), ks_got[:].rearrange("p (s r) -> p r s", r=PACK))
+        nc.sync.dma_start(ks_moved[0:100, :].bitcast(I32), ks_both[16:116, :].bitcast(I32))
         ks_dealt = [ks_both, ks_moved]
+        load_v(1, "ks_got")
         k_dealt = []
         k_halves = k_got[:].bitcast(U16).rearrange("p (a i r o) -> p o a r i", i=4, r=PACK, o=PASSES)
 
@@ -101,7 +102,9 @@ def tile_attend_plo_mlpsilu_topk_kernel(tc, qT, k_words, k_scales, vT, ob, us, o
 
         quantize_q(0, [nc.vector.tensor_copy, nc.vector.tensor_copy])
         split_k(1, "q_bf00")
+        load_v(2, None)
         quantize_q(1, [nc.vector.tensor_copy, nc.vector.tensor_copy])
+        load_v(3, "q_raw1")
 
         a_banks = [ps.tile([P, PACK, CHUNK], F32, name=f"a_bank{c}", tag=f"bank{c}") for c in range(CHUNKS)]
         for o in range(PASSES):
@@ -120,8 +123,8 @@ def tile_attend_plo_mlpsilu_topk_kernel(tc, qT, k_words, k_scales, vT, ob, us, o
 
         v_codes, v_scales = {}, {}
 
-        def gather_v(u, on_vector):
-            v_got = tile([P, SLOTS], BF16, f"v_got{u}")
+        def gather_v(u, on_vector, tag=None):
+            v_got = tile([P, SLOTS], BF16, f"v_got{u}", tag)
             if on_vector > 0:
                 nc.vector.tensor_copy(v_got[:, 0:on_vector], v_pool[u][:].indirect(offsets[:, 0 : on_vector // 16]))
             if on_vector < SLOTS:
@@ -142,8 +145,8 @@ def tile_attend_plo_mlpsilu_topk_kernel(tc, qT, k_words, k_scales, vT, ob, us, o
             for n, u in enumerate(us_here):
                 v_codes[u], v_scales[u] = codes[:, P * n : P * (n + 1)], scales[:, P * n : P * (n + 1)]
 
-        v_got0 = gather_v(0, SLOTS)
 
+        v_got0 = gather_v(0, SLOTS)
         y_bf = tile([P, NQ * PACK], BF16, "y_bf", "v_pool0")
         y_codes = tile([P, NQ], U32, "y_codes")
         y_scales = tile([P, NQ], U8, "y_scales")
@@ -185,7 +188,7 @@ def tile_attend_plo_mlpsilu_topk_kernel(tc, qT, k_words, k_scales, vT, ob, us, o
         turn_v(1, v_got1, v_bf12[:, 0 : 2 * P])
         turn_v(2, v_got2, v_bf12[:, 2 * P : 4 * P])
         v_got3 = gather_v(3, HALF)
-        quantize_v([1, 2], v_bf12, "v_pool3")
+        quantize_v([1, 2], v_bf12, "q_raw1")
         v_bf3 = tile([P, 2 * P], F32, "v_bf3")
         turn_v(3, v_got3, v_bf3[:])
         quantize_v([3], v_bf3)

@@ -42,14 +42,14 @@ def tile_attend_plo_mlpsilu_topk_kernel(tc, qT, k_words, k_scales, vT, ob, us, o
             engine_copy(dst.rearrange("p (c i) t -> p c t i", i=4), src.rearrange("p t (c i) -> p c t i", i=4))
 
         offsets = sb.tile([P, SLOTS // 16], U16, name="offsets")
-        nc.sync.dma_start(offsets[:], offs)
         k_pool = tile([P, TOKENS], I32, "k_pool")
         nc.sync.dma_start(k_pool[:], k_words[0].rearrange("p t b -> p (t b)").bitcast(I32))
+        nc.sync.dma_start(offsets[:], offs)
         ks_pool = tile([P, TOKENS], U8, "ks_pool")
         nc.vector.memset(ks_pool[:].bitcast(I32), 0)
         for j in range(4):
             nc.sync.dma_start(ks_pool[j:P:16, :].bitcast(I32), k_scales[:, j:16:4, :].rearrange("o f t -> f o t").bitcast(I32))
-        q_raw = [placed([P, PACK, NQ], F32, "q_raw0", 0), tile([P, PACK, NQ], F32, "q_raw1")]
+        q_raw = [placed([P, PACK, NQ], F32, f"q_raw{o}", 8192 * o) for o in range(PASSES)]
         q_rows = qT[0].rearrange("(o p j) w -> o p j w", o=PASSES, j=PACK)
         for o in range(PASSES):
             nc.sync.dma_start(q_raw[o][:], q_rows[o])
@@ -57,14 +57,14 @@ def tile_attend_plo_mlpsilu_topk_kernel(tc, qT, k_words, k_scales, vT, ob, us, o
         v_pool = {}
 
         def load_v(u, tag):
-            v_pool[u] = placed([P, TOKENS], F32, "v_pool2", 0) if u == 2 else tile([P, TOKENS], F32, f"v_pool{u}", tag)
+            v_pool[u] = placed([P, TOKENS], F32, f"v_pool{u}", 8192 * (u - 2)) if u >= 2 else tile([P, TOKENS], F32, f"v_pool{u}", tag)
             nc.sync.dma_start(v_pool[u][:], v_rows[:, u, :])
 
         load_v(0, None)
         us_t = tile([P, PACK], F32, "us_t")
-        nc.sync.dma_start(us_t[:], us[0].rearrange("(p r) o -> p (r o)", r=PACK))
+        nc.gpsimd.dma_start(us_t[:], us[0].rearrange("(p r) o -> p (r o)", r=PACK))
         ob_t = tile([P, PACK], F32, "ob_t")
-        nc.sync.dma_start(ob_t[:], ob[0].rearrange("(p r) o -> p (r o)", r=PACK))
+        nc.gpsimd.dma_start(ob_t[:], ob[0].rearrange("(p r) o -> p (r o)", r=PACK))
         ks_moved = tile([P, SLOTS], U8, "ks_moved")
         nc.gpsimd.memset(ks_moved[:].bitcast(I32), 0)
         ident = tile([P, P], F32, "ident")
@@ -104,7 +104,7 @@ def tile_attend_plo_mlpsilu_topk_kernel(tc, qT, k_words, k_scales, vT, ob, us, o
         split_k(1, "q_bf00")
         load_v(2, None)
         quantize_q(1, [nc.vector.tensor_copy, nc.vector.tensor_copy])
-        load_v(3, "q_raw1")
+        load_v(3, None)
 
         a_banks = [ps.tile([P, PACK, CHUNK], F32, name=f"a_bank{c}", tag=f"bank{c}") for c in range(CHUNKS)]
         for o in range(PASSES):
@@ -138,13 +138,11 @@ def tile_attend_plo_mlpsilu_topk_kernel(tc, qT, k_words, k_scales, vT, ob, us, o
                 nc.tensor.transpose(turned[:, h, :], words[:, h : SLOTS // 2 : 2], ident[:])
             nc.scalar.copy(v_bf.rearrange("p (m h) -> p m h", h=2), turned[:].rearrange("p h m -> p m h"))
 
-        def quantize_v(us_here, v_bf, tag=None):
-            codes = tile([P, P * len(us_here)], U32, f"v_codes{us_here[0]}", tag)
-            scales = tile([P, P * len(us_here)], U8, f"v_scales{us_here[0]}")
-            nc.vector.quantize_mx(out=codes[:].bitcast(FP8X4), scales=scales[:], in_=v_bf[:].bitcast(BF16))
-            for n, u in enumerate(us_here):
-                v_codes[u], v_scales[u] = codes[:, P * n : P * (n + 1)], scales[:, P * n : P * (n + 1)]
-
+        def quantize_v(u, v_bf, offset=None):
+            name = f"v_codes{u}"
+            v_codes[u] = tile([P, P], U32, name) if offset is None else placed([P, P], U32, name, offset)
+            v_scales[u] = tile([P, P], U8, f"v_scales{u}")
+            nc.vector.quantize_mx(out=v_codes[u][:].bitcast(FP8X4), scales=v_scales[u][:], in_=v_bf[:].bitcast(BF16))
 
         v_got0 = gather_v(0, SLOTS)
         y_bf = tile([P, NQ * PACK], BF16, "y_bf", "v_pool0")
@@ -161,13 +159,13 @@ def tile_attend_plo_mlpsilu_topk_kernel(tc, qT, k_words, k_scales, vT, ob, us, o
             nc.vector.quantize_mx(out=y_codes[:, cols].bitcast(FP8X4), scales=y_scales[:, cols],
                                   in_=y_bf[:, PACK * cols.start : PACK * cols.stop])
 
-        res = placed([P, PACK * NQ], F32, "res", 2048)
+        res = placed([P, PACK * NQ], F32, "res", 8192 + 1024)
         res_rows = res[:].rearrange("p (u q) -> p u q", u=PACK)
         out_rows = out_0.rearrange("(p u) q -> p u q", u=PACK)
 
         def second(u, cols, tag, on_vector):
             bank = ps.tile([P, cols.stop - cols.start], F32, name=f"o_bank{u}_{cols.start}", tag=tag)
-            nc.tensor.matmul_mx(out=bank[:], lhsT=v_codes[u].bitcast(FP8X4), lhsT_scale=v_scales[u],
+            nc.tensor.matmul_mx(out=bank[:], lhsT=v_codes[u][:].bitcast(FP8X4), lhsT_scale=v_scales[u][:],
                                 rhs=y_codes[:, cols].bitcast(FP8X4), rhs_scale=y_scales[:, cols], start=True, stop=True)
             if on_vector:
                 nc.vector.tensor_scalar(res[:, NQ * u + cols.start : NQ * u + cols.stop], bank[:], ob_t[:, u : u + 1], None, ALU.add)
@@ -180,34 +178,41 @@ def tile_attend_plo_mlpsilu_topk_kernel(tc, qT, k_words, k_scales, vT, ob, us, o
         whole = slice(0, NQ)
         v_bf0 = tile([P, 2 * P], F32, "v_bf0")
         turn_v(0, v_got0, v_bf0[:])
-        quantize_v([0], v_bf0)
+        quantize_v(0, v_bf0)
         v_got2 = gather_v(2, HALF)
-        second(0, whole, "bank4", True)
-        store(0)
-        v_bf12 = placed([P, 4 * P], F32, "v_bf12", 0)
-        turn_v(1, v_got1, v_bf12[:, 0 : 2 * P])
-        turn_v(2, v_got2, v_bf12[:, 2 * P : 4 * P])
+        v_bf1 = placed([P, 2 * P], F32, "v_bf1", 0)
+        turn_v(1, v_got1, v_bf1[:])
+        quantize_v(1, v_bf1)
+        v_bf2 = tile([P, 2 * P], F32, "v_bf2")
+        turn_v(2, v_got2, v_bf2[:])
         v_got3 = gather_v(3, HALF)
-        quantize_v([1, 2], v_bf12, "q_raw1")
+        quantize_v(2, v_bf2, 8192)
+        second(0, whole, "bank4", False)
+        store(0)
         v_bf3 = tile([P, 2 * P], F32, "v_bf3")
         turn_v(3, v_got3, v_bf3[:])
-        quantize_v([3], v_bf3)
-        second(1, whole, "bank5", False)
+        second(1, whole, "bank5", True)
         store(1)
-        second(2, whole, "bank1", True)
+        quantize_v(3, v_bf3)
+        second(2, whole, "bank1", False)
         store(2)
         second(3, slice(0, HALF), "bank2", False)
-        second(3, slice(HALF, NQ), "bank3", True)
+        second(3, slice(HALF, NQ), "bank3", False)
         store(3)
 
         res_bf = tile([P, NQ, PACK], BF16, "res_bf")
         o_codes = tile([P, NQ], I32, "o_codes")
         o_scales = tile([P, NQ], U8, "o_scales")
+        split = 352
         weave(nc.vector.tensor_copy, res_bf[:, 0:HALF, :], res_rows[:, :, 0:HALF])
-        weave(nc.vector.tensor_copy, res_bf[:, HALF : HALF + CHUNK, :], res_rows[:, :, HALF : HALF + CHUNK])
-        weave(nc.scalar.copy, res_bf[:, HALF + CHUNK : NQ, :], res_rows[:, :, HALF + CHUNK : NQ])
-        nc.vector.quantize_mx(out=o_codes[:].bitcast(FP8X4), scales=o_scales[:], in_=res_bf[:].rearrange("p n t -> p (n t)"))
-        nc.sync.dma_start(out_1[0].rearrange("p q b -> p (q b)").bitcast(I32), o_codes[:])
+        weave(nc.vector.tensor_copy, res_bf[:, HALF:split, :], res_rows[:, :, HALF:split])
+        weave(nc.scalar.copy, res_bf[:, split:NQ, :], res_rows[:, :, split:NQ])
+        words_out = out_1[0].rearrange("p q b -> p (q b)").bitcast(I32)
+        for h in range(2):
+            cols = slice(HALF * h, HALF * (h + 1))
+            nc.vector.quantize_mx(out=o_codes[:, cols].bitcast(FP8X4), scales=o_scales[:, cols],
+                                  in_=res_bf[:, cols, :].rearrange("p n t -> p (n t)"))
+            nc.sync.dma_start(words_out[:, cols], o_codes[:, cols])
         for j in range(4):
-            engine = nc.scalar if j % 2 else nc.sync
+            engine = nc.sync if j == 3 else nc.scalar
             engine.dma_start(out_2[0, j:16:4, :].bitcast(I32), o_scales[j:P:32, :].bitcast(I32))

from contextlib import ExitStack

import concourse.mybir as mybir
from concourse.masks import make_identity

F32 = mybir.dt.float32
BF16 = mybir.dt.bfloat16
I32 = mybir.dt.int32
U32 = mybir.dt.uint32
U16 = mybir.dt.uint16
U8 = mybir.dt.uint8
FP8X4 = mybir.dt.float8_e4m3fn_x4
FP4X4 = mybir.dt.float4_e2m1fn_x4
ACT = mybir.ActivationFunctionType
ALU = mybir.AluOpType

P = 128
PACK = 4
SLOTS, TOKENS, D, NQ, DV = 512, 2048, 1024, 512, 512
PASSES = D // (P * PACK)
CHUNK = 128
CHUNKS = NQ // CHUNK
HALF = NQ // 2

FLOPS = 2 * SLOTS * NQ * (D + DV)


def tile_attend_plo_mlpsilu_topk_kernel(tc, qT, k_words, k_scales, vT, ob, us, offs, out_0, out_1, out_2):
    nc = tc.nc
    with ExitStack() as ctx:
        sb = ctx.enter_context(tc.tile_pool(name="sb", bufs=1))
        reuse = ctx.enter_context(tc.tile_pool(name="reuse", bufs=1))
        ps = ctx.enter_context(tc.psum_pool(name="ps", bufs=1))

        def tile(shape, dtype, name, tag=None):
            return sb.tile(shape, dtype, name=name, tag=tag or name, align_bytes=64)

        def placed(shape, dtype, name, offset):
            return reuse.tile(shape, dtype, name=name, align_bytes=64, offset=offset)

        def weave(engine_copy, dst, src):
            engine_copy(dst.rearrange("p (c i) t -> p c t i", i=4), src.rearrange("p t (c i) -> p c t i", i=4))

        offsets = sb.tile([P, SLOTS // 16], U16, name="offsets")
        k_pool = tile([P, TOKENS], I32, "k_pool")
        nc.sync.dma_start(k_pool[:], k_words[0].rearrange("p t b -> p (t b)").bitcast(I32))
        nc.sync.dma_start(offsets[:], offs)
        ks_pool = tile([P, TOKENS], U8, "ks_pool")
        nc.vector.memset(ks_pool[:].bitcast(I32), 0)
        for j in range(4):
            nc.sync.dma_start(ks_pool[j:P:16, :].bitcast(I32), k_scales[:, j:16:4, :].rearrange("o f t -> f o t").bitcast(I32))
        q_raw = [placed([P, PACK, NQ], F32, f"q_raw{o}", 8192 * o) for o in range(PASSES)]
        q_rows = qT[0].rearrange("(o p j) w -> o p j w", o=PASSES, j=PACK)
        for o in range(PASSES):
            nc.sync.dma_start(q_raw[o][:], q_rows[o])
        v_rows = vT.rearrange("(p u) t -> p u t", u=PACK)
        v_pool = {}

        def load_v(u, tag):
            v_pool[u] = placed([P, TOKENS], F32, f"v_pool{u}", 8192 * (u - 2)) if u >= 2 else tile([P, TOKENS], F32, f"v_pool{u}", tag)
            nc.sync.dma_start(v_pool[u][:], v_rows[:, u, :])

        load_v(0, None)
        us_t = tile([P, PACK], F32, "us_t")
        nc.gpsimd.dma_start(us_t[:], us[0].rearrange("(p r) o -> p (r o)", r=PACK))
        ob_t = tile([P, PACK], F32, "ob_t")
        nc.gpsimd.dma_start(ob_t[:], ob[0].rearrange("(p r) o -> p (r o)", r=PACK))
        ks_moved = tile([P, SLOTS], U8, "ks_moved")
        nc.gpsimd.memset(ks_moved[:].bitcast(I32), 0)
        ident = tile([P, P], F32, "ident")
        make_identity(nc, ident[:])

        k_got = tile([P, SLOTS], I32, "k_got")
        nc.vector.tensor_copy(k_got[:].bitcast(U32), k_pool[:].bitcast(U32).indirect(offsets[:]))
        ks_got = tile([P, SLOTS], U8, "ks_got")
        nc.vector.tensor_copy(ks_got[:], ks_pool[:].indirect(offsets[:]))
        ks_both = tile([P, SLOTS], U8, "ks_both")
        nc.vector.tensor_copy(ks_both[:].rearrange("p (r s) -> p r s", r=PACK), ks_got[:].rearrange("p (s r) -> p r s", r=PACK))
        nc.sync.dma_start(ks_moved[0:100, :].bitcast(I32), ks_both[16:116, :].bitcast(I32))
        ks_dealt = [ks_both, ks_moved]
        load_v(1, "ks_got")
        k_dealt = []
        k_halves = k_got[:].bitcast(U16).rearrange("p (a i r o) -> p o a r i", i=4, r=PACK, o=PASSES)

        def split_k(o, tag):
            k_dealt.append(tile([P, 2 * SLOTS], U8, f"k_dealt{o}", tag))
            nc.vector.tensor_copy(k_dealt[o][:].bitcast(U16).rearrange("p (r a i) -> p a r i", r=PACK, i=4), k_halves[:, o])

        split_k(0, "ks_pool")

        q_codes, q_scales = {}, {}

        def quantize_q(o, copies):
            q_bf = [tile([P, HALF, PACK], BF16, f"q_bf{o}{h}") for h in range(2)]
            for h in range(2):
                weave(copies[h], q_bf[h][:], q_raw[o][:, :, HALF * h : HALF * (h + 1)])
            for h in range(2):
                q_codes[o, h] = tile([P, HALF], U32, f"q_codes{o}{h}")
                q_scales[o, h] = tile([P, HALF], U8, f"q_scales{o}{h}")
                nc.vector.quantize_mx(out=q_codes[o, h][:].bitcast(FP8X4), scales=q_scales[o, h][:],
                                      in_=q_bf[h][:].rearrange("p n t -> p (n t)"))

        quantize_q(0, [nc.vector.tensor_copy, nc.vector.tensor_copy])
        split_k(1, "q_bf00")
        load_v(2, None)
        quantize_q(1, [nc.vector.tensor_copy, nc.vector.tensor_copy])
        load_v(3, None)

        a_banks = [ps.tile([P, PACK, CHUNK], F32, name=f"a_bank{c}", tag=f"bank{c}") for c in range(CHUNKS)]
        for o in range(PASSES):
            for c in range(CHUNKS):
                h, cols = c // 2, slice(CHUNK * (c % 2), CHUNK * (c % 2 + 1))
                for r in range(PACK):
                    nc.tensor.matmul_mx(
                        out=a_banks[c][:, r, :],
                        lhsT=k_dealt[o][:, 2 * P * r : 2 * P * (r + 1)].bitcast(FP4X4),
                        lhsT_scale=ks_dealt[o][:, P * r : P * (r + 1)],
                        rhs=q_codes[o, h][:, cols].bitcast(FP8X4),
                        rhs_scale=q_scales[o, h][:, cols],
                        start=(o == 0 and r == 0),
                        stop=(o == PASSES - 1 and r == PACK - 1),
                    )

        v_codes, v_scales = {}, {}

        def gather_v(u, on_vector, tag=None):
            v_got = tile([P, SLOTS], BF16, f"v_got{u}", tag)
            if on_vector > 0:
                nc.vector.tensor_copy(v_got[:, 0:on_vector], v_pool[u][:].indirect(offsets[:, 0 : on_vector // 16]))
            if on_vector < SLOTS:
                nc.scalar.activation(v_got[:, on_vector:SLOTS], v_pool[u][:].indirect(offsets[:, on_vector // 16 : SLOTS // 16]), ACT.Copy)
            return v_got

        def turn_v(u, v_got, v_bf):
            words = v_got[:].bitcast(F32)
            turned = ps.tile([P, 2, P], F32, name=f"turned{u}", tag=("bank0", "bank6", "bank7", "bank6")[u])
            for h in range(2):
                nc.tensor.transpose(turned[:, h, :], words[:, h : SLOTS // 2 : 2], ident[:])
            nc.scalar.copy(v_bf.rearrange("p (m h) -> p m h", h=2), turned[:].rearrange("p h m -> p m h"))

        def quantize_v(u, v_bf, offset=None):
            name = f"v_codes{u}"
            v_codes[u] = tile([P, P], U32, name) if offset is None else placed([P, P], U32, name, offset)
            v_scales[u] = tile([P, P], U8, f"v_scales{u}")
            nc.vector.quantize_mx(out=v_codes[u][:].bitcast(FP8X4), scales=v_scales[u][:], in_=v_bf[:].bitcast(BF16))

        v_got0 = gather_v(0, SLOTS)
        y_bf = tile([P, NQ * PACK], BF16, "y_bf", "v_pool0")
        y_codes = tile([P, NQ], U32, "y_codes")
        y_scales = tile([P, NQ], U8, "y_scales")
        us_wide = us_t[:].unsqueeze(1).to_broadcast([P, CHUNK, PACK])
        for c in range(CHUNKS):
            act = tile([P, CHUNK, PACK], F32, f"act{c}")
            nc.scalar.activation(act[:], a_banks[c][:].rearrange("p r n -> p n r"), ACT.Silu)
            nc.vector.tensor_tensor(y_bf[:, PACK * CHUNK * c : PACK * CHUNK * (c + 1)].rearrange("p (n t) -> p n t", t=PACK), act[:], us_wide, ALU.mult)
        v_got1 = gather_v(1, 0)
        for h in range(2):
            cols = slice(HALF * h, HALF * (h + 1))
            nc.vector.quantize_mx(out=y_codes[:, cols].bitcast(FP8X4), scales=y_scales[:, cols],
                                  in_=y_bf[:, PACK * cols.start : PACK * cols.stop])

        res = placed([P, PACK * NQ], F32, "res", 8192 + 1024)
        res_rows = res[:].rearrange("p (u q) -> p u q", u=PACK)
        out_rows = out_0.rearrange("(p u) q -> p u q", u=PACK)

        def second(u, cols, tag, on_vector):
            bank = ps.tile([P, cols.stop - cols.start], F32, name=f"o_bank{u}_{cols.start}", tag=tag)
            nc.tensor.matmul_mx(out=bank[:], lhsT=v_codes[u][:].bitcast(FP8X4), lhsT_scale=v_scales[u][:],
                                rhs=y_codes[:, cols].bitcast(FP8X4), rhs_scale=y_scales[:, cols], start=True, stop=True)
            if on_vector:
                nc.vector.tensor_scalar(res[:, NQ * u + cols.start : NQ * u + cols.stop], bank[:], ob_t[:, u : u + 1], None, ALU.add)
            else:
                nc.scalar.activation(res[:, NQ * u + cols.start : NQ * u + cols.stop], bank[:], ACT.Identity, bias=ob_t[:, u : u + 1])

        def store(u):
            nc.sync.dma_start(out_rows[:, u, :], res[:, u * NQ : (u + 1) * NQ])

        whole = slice(0, NQ)
        v_bf0 = tile([P, 2 * P], F32, "v_bf0")
        turn_v(0, v_got0, v_bf0[:])
        quantize_v(0, v_bf0)
        v_got2 = gather_v(2, HALF)
        v_bf1 = placed([P, 2 * P], F32, "v_bf1", 0)
        turn_v(1, v_got1, v_bf1[:])
        quantize_v(1, v_bf1)
        v_bf2 = tile([P, 2 * P], F32, "v_bf2")
        turn_v(2, v_got2, v_bf2[:])
        v_got3 = gather_v(3, HALF)
        quantize_v(2, v_bf2, 8192)
        second(0, whole, "bank4", False)
        store(0)
        v_bf3 = tile([P, 2 * P], F32, "v_bf3")
        turn_v(3, v_got3, v_bf3[:])
        second(1, whole, "bank5", True)
        store(1)
        quantize_v(3, v_bf3)
        second(2, whole, "bank1", False)
        store(2)
        second(3, slice(0, HALF), "bank2", False)
        second(3, slice(HALF, NQ), "bank3", False)
        store(3)

        res_bf = tile([P, NQ, PACK], BF16, "res_bf")
        o_codes = tile([P, NQ], I32, "o_codes")
        o_scales = tile([P, NQ], U8, "o_scales")
        split = 352
        weave(nc.vector.tensor_copy, res_bf[:, 0:HALF, :], res_rows[:, :, 0:HALF])
        weave(nc.vector.tensor_copy, res_bf[:, HALF:split, :], res_rows[:, :, HALF:split])
        weave(nc.scalar.copy, res_bf[:, split:NQ, :], res_rows[:, :, split:NQ])
        words_out = out_1[0].rearrange("p q b -> p (q b)").bitcast(I32)
        for h in range(2):
            cols = slice(HALF * h, HALF * (h + 1))
            nc.vector.quantize_mx(out=o_codes[:, cols].bitcast(FP8X4), scales=o_scales[:, cols],
                                  in_=res_bf[:, cols, :].rearrange("p n t -> p (n t)"))
            nc.sync.dma_start(words_out[:, cols], o_codes[:, cols])
        for j in range(4):
            engine = nc.sync if j == 3 else nc.scalar
            engine.dma_start(out_2[0, j:16:4, :].bitcast(I32), o_scales[j:P:32, :].bitcast(I32))
